import numpy as np
import ml_dtypes


def mxq(x, axis, fmt="e4m3"):
    dtype, down = {"e4m3": (ml_dtypes.float8_e4m3fn, 7), "e5m2": (ml_dtypes.float8_e5m2, 14)}[fmt]
    v = np.moveaxis(np.asarray(x, np.float32).astype(ml_dtypes.bfloat16).astype(np.float64), axis, -1)
    blocks = v.reshape(v.shape[:-1] + (-1, 32))
    amax = np.abs(blocks).max(-1, keepdims=True)
    byte = np.maximum(np.where(amax > 0, np.frexp(amax)[1] - 1 + 127, 0) - down, 1)
    scale = np.exp2(byte - 127.0)
    codes = (blocks / scale).astype(np.float32).astype(dtype).astype(np.float64)
    return np.moveaxis((codes * scale).reshape(v.shape), -1, axis)


WIDE = False


def mx_kscale(k):
    if not WIDE:
        return np.ones(k)
    levels = np.array([10, -10, 5, -5, 0])
    if k % 512:
        return np.exp2(np.random.permutation(np.resize(levels, k // 32))).repeat(32)
    a = np.empty((k // 512, 16))
    for p in range(k // 512):
        a[p, :8] = np.random.permutation(np.resize(levels, 8))
        for g in range(8):
            far = levels[np.abs(levels - a[p, g]) >= 10]
            a[p, g + 8] = far[np.random.randint(len(far))]
    return np.exp2(a.ravel()).repeat(32)


def f64(x):
    return np.asarray(x).astype(np.float64)


def striped(idx):
    return np.tile(idx.reshape(-1, 16).T, (8, 1)).astype(np.uint16)


def unstriped(offs):
    return offs[:16].T.reshape(-1).astype(np.int64)


def striped8(idx):
    return np.concatenate([x.reshape(-1, 16).T for x in idx]).astype(np.uint16)


def runs(offs, k):
    lists = np.stack([offs[16 * r : 16 * r + 16].T.reshape(-1) for r in range(8)]).astype(np.int64)
    return lists[np.arange(k) % 512 // 64]


def pack_weight(w):
    k, n = w.shape
    w = f64(np.asarray(w, np.float32).astype(ml_dtypes.bfloat16)).reshape(k // 32, 32, n)
    amax = np.abs(w).max(1)
    byte = np.clip(np.where(amax > 0, np.frexp(amax)[1] - 1 + 127 - 7, 1), 1, 254)
    scaled = (w * np.exp2(127.0 - byte)[:, None, :]).reshape(k, n).astype(np.float32)
    words = np.ascontiguousarray(scaled.reshape(k // 512, 128, 4, n).transpose(0, 1, 3, 2)).astype(ml_dtypes.float8_e4m3fn).view(np.uint8)
    return words, np.ascontiguousarray(byte.astype(np.uint8).reshape(k // 512, 16, n))


def unpack_weight(words, scales):
    g, p, n, _ = words.shape
    vals = np.ascontiguousarray(words).view(ml_dtypes.float8_e4m3fn).astype(np.float64) * np.repeat(np.exp2(scales.astype(np.float64) - 127.0), 8, axis=1)[..., None]
    return vals.transpose(0, 1, 3, 2).reshape(g * 512, n)


K, T, S, H = 512, 2048, 512, 512


def setup_inputs():
    n = np.random.standard_normal
    s = mx_kscale(K)[:, None]
    u = mx_kscale(S)
    packed_xT = pack_weight(n((K, T)) * s)
    return {
        "x_words": packed_xT[0],
        "x_scales": packed_xT[1],
        "w1": (n((K, H)) / np.sqrt(K) / s).astype(np.float32),
        "ga": (np.random.uniform(0.5, 1.5, (H, 1)) * u[:, None]).astype(np.float32),
        "gb": (np.random.uniform(0.5, 1.5, (H, 1)) / u[:, None]).astype(np.float32),
        "offs": striped(np.random.permutation(T)[:S]),
        "n1": striped8(np.stack([np.random.permutation(S) for _ in range(8)])),
        "n2": striped8(np.stack([np.random.permutation(S) for _ in range(8)])),
        "n3": striped8(np.stack([np.random.permutation(S) for _ in range(8)])),
        "n4": striped8(np.stack([np.random.permutation(S) for _ in range(8)])),
        "n5": striped8(np.stack([np.random.permutation(S) for _ in range(8)])),
        "n6": striped8(np.stack([np.random.permutation(S) for _ in range(8)])),
    }


def reference(x_words, x_scales, w1, ga, gb, offs, n1, n2, n3, n4, n5, n6):
    xq = unpack_weight(x_words, x_scales)[:, unstriped(offs)]
    y = mxq(f64(w1), 0, "e4m3").T @ xq
    pa = y[np.arange(H)[:, None], runs(n1, H)]
    kr = np.exp(-0.5 * ((y - pa) ** 2))
    pb = y[np.arange(H)[:, None], runs(n2, H)]
    kr2 = np.exp(-0.5 * ((y - pb) ** 2))
    z = f64(ga) * ((kr * pa + kr2 * pb) / (kr + kr2 + 0.5))
    z2 = f64(gb) * ((y - (y[np.arange(H)[:, None], runs(n3, H)])) / (np.abs(y[np.arange(H)[:, None], runs(n4, H)] - y) + 0.5))
    s = 0.0625 * ((mxq(z, 0, "e4m3").T @ mxq(z2, 0, "e4m3")))
    return s - (np.minimum(s[np.arange(S)[:, None], runs(n5, S)], s[np.arange(S)[:, None], runs(n6, S)]))

@@ -1,0 +1,263 @@
+from contextlib import ExitStack
+
+import concourse.mybir as mybir
+from concourse.masks import make_identity
+
+F32 = mybir.dt.float32
+BF16 = mybir.dt.bfloat16
+I32 = mybir.dt.int32
+U32 = mybir.dt.uint32
+U16 = mybir.dt.uint16
+U8 = mybir.dt.uint8
+FP8X4 = mybir.dt.float8_e4m3fn_x4
+ALU = mybir.AluOpType
+ACT = mybir.ActivationFunctionType
+
+P = 128
+T = 2048
+S = 512
+WINDOW = 1024
+FLOPS = 2 * 2 * 512 * 512 * 512
+PE_DIFF = ((True, True), (True, True), (True, True), (True, True))
+
+
+def tile_picked_selfkernfracunder_none_p_kernel(
+    tc, x_words, x_scales, w1, ga, gb, offs, n1, n2, n3, n4, n5, n6, out
+):
+    nc = tc.nc
+    with ExitStack() as ctx:
+        keep = ctx.enter_context(tc.tile_pool(name="keep", bufs=1))
+        ring = ctx.enter_context(tc.tile_pool(name="ring", bufs=2))
+        psum = ctx.enter_context(tc.psum_pool(name="psum", bufs=2))
+
+        def load_list(name, src):
+            tile = keep.tile([P, S // 16], U16, name=name)
+            nc.sync.dma_start(tile[:], src)
+            return tile
+
+        def load_gain(name, src):
+            cols = []
+            for t in range(4):
+                col = keep.tile([P, 1], F32, name="%s%d" % (name, t))
+                with nc.allow_non_contiguous_dma(reason="one value a partition"):
+                    nc.sync.dma_start(col[:], src.rearrange("(g t a) o -> t g a o", t=4, a=8)[t])
+                cols.append(col)
+            return cols
+
+        def flip(bank, terms):
+            for c in range(4):
+                cols = slice(c * P, (c + 1) * P)
+                for i, term in enumerate(terms):
+                    nc.tensor.matmul(bank[:, cols], term[:, cols], ident[:], is_transpose=True,
+                                     start=(i == 0), stop=(i == len(terms) - 1))
+
+        def flip_block(bank, b, terms_of_t):
+            for t in range(4):
+                terms = terms_of_t[t]
+                for i, term in enumerate(terms):
+                    nc.tensor.matmul(bank[:, t * P:(t + 1) * P], term[:, b * P:(b + 1) * P], ident[:], is_transpose=True,
+                                     start=(i == 0), stop=(i == len(terms) - 1))
+
+        xs = keep.tile([P, T], U8, name="xs")
+        nc.gpsimd.memset(xs[:].bitcast(I32), 0)
+        l_offs = load_list("l_offs", offs)
+        for q in range(4):
+            nc.sync.dma_start(xs[32 * q:32 * q + 4, :].bitcast(I32), x_scales[0, 4 * q:4 * q + 4, :].bitcast(I32))
+        w_raw = keep.tile([P, 4, S], F32, name="w_raw")
+        nc.sync.dma_start(w_raw[:], w1.rearrange("(p j) c -> p j c", j=4))
+        xw = keep.tile([P, T], I32, name="xw")
+        nc.sync.dma_start(xw[:], x_words[0].rearrange("p n t -> p (n t)").bitcast(I32))
+        l1 = load_list("l1", n1)
+        l2 = load_list("l2", n2)
+        l4 = load_list("l4", n4)
+        l3 = load_list("l3", n3)
+        ga_t = load_gain("ga", ga)
+        gb_t = load_gain("gb", gb)
+        l5 = load_list("l5", n5)
+        l6 = load_list("l6", n6)
+
+        ident = keep.tile([P, P], F32, name="ident")
+        make_identity(nc, ident[:])
+        win = [keep.tile([P, WINDOW], F32, name="win%d" % t) for t in range(4)]
+        for t in range(4):
+            nc.vector.memset(win[t][:, S:], 0.0)
+
+        xq_s = keep.tile([P, S], U8, name="xq_s", align_bytes=64)
+        nc.vector.tensor_copy(xq_s[:], xs[:].indirect(l_offs[:]))
+        w_c, w_s = [], []
+        w_view = w_raw[:].rearrange("p j (g t a) -> p t g a j", t=4, a=8)
+        for t in range(4):
+            wg = keep.tile([P, S], BF16, name="wg%d" % t, align_bytes=64)
+            dst = wg[:].rearrange("p (g a j) -> p g a j", a=8, j=4)
+            if t < 2:
+                nc.vector.tensor_copy(dst, w_view[:, t])
+            else:
+                nc.scalar.activation(dst, w_view[:, t], ACT.Copy)
+            w_c.append(keep.tile([P, P], U32, name="w_c%d" % t, align_bytes=64))
+            w_s.append(keep.tile([P, P], U8, name="w_s%d" % t, align_bytes=64))
+            nc.vector.quantize_mx(out=w_c[t][:].bitcast(FP8X4), scales=w_s[t][:], in_=wg[:])
+        xq = keep.tile([P, S], U32, name="xq", align_bytes=64)
+        for h in range(2):
+            nc.vector.tensor_copy(xq[:, h * 256:(h + 1) * 256], xw[:].bitcast(U32).indirect(l_offs[:, h * 16:(h + 1) * 16]))
+
+        y_plain = [keep.tile([P, S], F32, name="y_plain%d" % t) for t in range(4)]
+        for t in range(4):
+            width = 256 if t == 0 else S
+            for c0 in range(0, S, width):
+                cols = slice(c0, c0 + width)
+                acc = psum.tile([P, S], F32, name="acc", tag="acc")
+                nc.tensor.matmul_mx(out=acc[:, :width], lhsT=w_c[t][:].bitcast(FP8X4), lhsT_scale=w_s[t][:],
+                                    rhs=xq[:, cols].bitcast(FP8X4), rhs_scale=xq_s[:, cols], start=True, stop=True)
+                nc.scalar.activation(win[t][:, cols], acc[:, :width], ACT.Copy)
+            nc.sync.dma_start(y_plain[t][:], win[t][:, :S])
+
+        neg = [[keep.tile([P, S], F32, name="neg%d_%d" % (t, i)) for i in range(2)] for t in range(4)]
+        kr = [[keep.tile([P, S], F32, name="kr%d_%d" % (t, i)) for i in range(2)] for t in range(4)]
+        for t in range(4):
+            for i, lst in enumerate((l1, l2)):
+                nc.vector.tensor_scalar(neg[t][i][:], win[t][:].indirect(lst[:]), -1.0, 0.0, ALU.mult, ALU.add)
+                if t == 3 and i == 1:
+                    sq = keep.tile([P, S], F32, name="sq_last", tag="late")
+                else:
+                    sq = ring.tile([P, S], F32, name="sq")
+                dealt = kr[t][i][:].rearrange("p (b g a) -> p b g a", b=4, a=8)
+                if PE_DIFF[t][i]:
+                    diff = psum.tile([P, S], F32, name="diff", tag="diff")
+                    flip(diff, (neg[t][i], win[t]))
+                    nc.scalar.activation(sq[:], diff[:], ACT.Square)
+                    back = psum.tile([P, S], F32, name="back", tag="back")
+                    flip(back, (sq,))
+                    src = back
+                else:
+                    dv = ring.tile([P, S], F32, name="dv")
+                    nc.vector.tensor_tensor(dv[:], neg[t][i][:], win[t][:, :S], ALU.add)
+                    nc.scalar.activation(sq[:], dv[:], ACT.Square)
+                    src = sq
+                nc.scalar.activation(dealt, src[:].rearrange("p (g b a) -> p b g a", b=4, a=8), ACT.Exp, scale=-0.5)
+
+        gap = keep.tile([P, 4, S], F32, name="gap")
+        for t in range(4):
+            d4 = ring.tile([P, S], F32, name="d4")
+            nc.vector.tensor_tensor(d4[:], win[t][:].indirect(l4[:]), y_plain[t][:], ALU.subtract)
+            nc.scalar.activation(gap[:, t, :], d4[:], ACT.Abs)
+        d3 = [keep.tile([P, S], F32, name="d3_%d" % t) for t in range(4)]
+        for t in range(4):
+            nc.vector.tensor_tensor(d3[t][:], win[t][:].indirect(l3[:]), y_plain[t][:], ALU.subtract)
+
+        prod = [[keep.tile([P, S], F32, name="prod%d_%d" % (t, i)) for i in range(2)] for t in range(4)]
+
+        def products(b):
+            for t in range(4):
+                for i in range(2):
+                    nc.vector.scalar_tensor_tensor(
+                        prod[t][i][:, b * P:(b + 1) * P].rearrange("p (g a) -> p g a", a=8),
+                        neg[t][i][:].rearrange("p (g b a) -> p b g a", b=4, a=8)[:, b],
+                        ga_t[t][:],
+                        kr[t][i][:, b * P:(b + 1) * P].rearrange("p (g a) -> p g a", a=8),
+                        ALU.mult, ALU.mult)
+
+        root2 = keep.tile([P, 4, S], F32, name="root2", tag="late")
+        z2_planes = keep.tile([P, 4, S], BF16, name="z2_planes")
+
+        def second_factor(t):
+            nc.scalar.activation(root2[:, t, :], gap[:, t, :], ACT.Abs_reciprocal_sqrt, bias=0.5)
+            inv2 = ring.tile([P, S], F32, name="inv2")
+            nc.scalar.activation(inv2[:], root2[:, t, :], ACT.Square)
+            nc.vector.scalar_tensor_tensor(z2_planes[:, t, :], d3[t][:], gb_t[t][:], inv2[:], ALU.mult, ALU.mult)
+
+        inv = [None] * 4
+
+        def inverse(b):
+            den = psum.tile([P, S], F32, name="den", tag="diff")
+            flip_block(den, b, kr)
+            root = ring.tile([P, S], F32, name="root")
+            nc.scalar.activation(root[:].rearrange("q (u p e) -> q u p e", u=2, e=2),
+                                 den[:].rearrange("q (u e p) -> q u p e", u=2, e=2), ACT.Abs_reciprocal_sqrt, bias=0.5)
+            inv[b] = ring.tile([P, S], F32, name="inv")
+            nc.scalar.activation(inv[b][:], root[:], ACT.Square)
+
+        z_c = [keep.tile([P, P], U32, name="z_c%d" % b, align_bytes=64) for b in range(4)]
+        z_s = [keep.tile([P, P], U8, name="z_s%d" % b, align_bytes=64) for b in range(4)]
+        z_g = [None] * 4
+
+        def first_factor(b):
+            num = psum.tile([P, S], F32, name="num", tag="back")
+            flip_block(num, b, prod)
+            z_t = ring.tile([P, S], BF16, name="z_t")
+            nc.vector.tensor_tensor(z_t[:].rearrange("q (u p e) -> q u p e", u=2, e=2),
+                                    num[:].rearrange("q (u e p) -> q u p e", u=2, e=2),
+                                    inv[b][:].rearrange("q (u p e) -> q u p e", u=2, e=2), ALU.mult)
+            pairs = psum.tile([P, S], F32, name="pairs", tag="pairs")
+            words = z_t[:].bitcast(F32)
+            for u in range(2):
+                nc.tensor.transpose(pairs[:, u * P:(u + 1) * P], words[:, u * P:(u + 1) * P], ident[:])
+            z_g[b] = ring.tile([P, S], BF16, name="z_g", align_bytes=64)
+            nc.scalar.copy(z_g[b][:].bitcast(F32).rearrange("p (j u) -> p j u", u=2),
+                           pairs[:, :2 * P].rearrange("p (u j) -> p j u", u=2))
+
+        def quantise_first(b):
+            nc.vector.quantize_mx(out=z_c[b][:].bitcast(FP8X4), scales=z_s[b][:], in_=z_g[b][:])
+
+        products(0)
+        second_factor(0)
+        second_factor(1)
+        second_factor(2)
+        second_factor(3)
+        inverse(0)
+        z2_g = keep.tile([P, S * 4], BF16, name="z2_g", align_bytes=64)
+        z2_c = keep.tile([P, S], U32, name="z2_c", align_bytes=64)
+        z2_s = keep.tile([P, S], U8, name="z2_s", align_bytes=64)
+        first_factor(0)
+        for h in range(2):
+            nc.scalar.copy(
+                z2_g[:, h * 1024:(h + 1) * 1024].rearrange("p (c i t) -> p c t i", i=4, t=4),
+                z2_planes[:, :, h * 256:(h + 1) * 256].rearrange("p t (c i) -> p c t i", i=4))
+        products(1)
+        quantise_first(0)
+        for h in range(2):
+            nc.vector.quantize_mx(out=z2_c[:, h * 256:(h + 1) * 256].bitcast(FP8X4), scales=z2_s[:, h * 256:(h + 1) * 256],
+                                  in_=z2_g[:, h * 1024:(h + 1) * 1024])
+
+        s_plain = [None] * 4
+        out_rows = out.rearrange("(g b a) n -> b g a n", b=4, a=8)
+
+        def second_product(b):
+            acc = psum.tile([P, S], F32, name="acc2", tag="acc")
+            nc.tensor.matmul_mx(out=acc[:], lhsT=z_c[b][:].bitcast(FP8X4), lhsT_scale=z_s[b][:],
+                                rhs=z2_c[:].bitcast(FP8X4), rhs_scale=z2_s[:], start=True, stop=True)
+            nc.scalar.activation(win[b][:, :S], acc[:], ACT.Copy, scale=-0.0625)
+            s_plain[b] = ring.tile([P, S], F32, name="s_plain")
+            nc.scalar.activation(s_plain[b][:], acc[:], ACT.Copy, scale=0.0625)
+
+        def finish(b, pieces):
+            width = S // pieces
+            for h in range(pieces):
+                cols = slice(h * width, (h + 1) * width)
+                lcols = slice(h * width // 16, (h + 1) * width // 16)
+                f5 = ring.tile([P, width], F32, name="f5")
+                f6 = ring.tile([P, width], F32, name="f6")
+                res = ring.tile([P, width], F32, name="res", bufs=3)
+                nc.vector.tensor_tensor(f5[:], win[b][:].indirect(l5[:, lcols]), s_plain[b][:, cols], ALU.add)
+                nc.vector.tensor_tensor(f6[:], win[b][:].indirect(l6[:, lcols]), s_plain[b][:, cols], ALU.add)
+                nc.vector.tensor_tensor(res[:], f5[:], f6[:], ALU.max)
+                nc.sync.dma_start(out_rows[b][:, :, cols], res[:])
+
+        second_product(0)
+        inverse(1)
+        first_factor(1)
+        products(2)
+        quantise_first(1)
+        second_product(1)
+        inverse(2)
+        finish(0, 1)
+        first_factor(2)
+        products(3)
+        quantise_first(2)
+        second_product(2)
+        inverse(3)
+        finish(1, 1)
+        first_factor(3)
+        quantise_first(3)
+        second_product(3)
+        finish(2, 1)
+        finish(3, 2)

@@ -18,6 +18,7 @@ T = 2048
 S = 512
 WINDOW = 1024
 FLOPS = 2 * 2 * 512 * 512 * 512
+PROD_BUFS = 1
 PE_DIFF = ((True, True), (True, True), (True, True), (True, True))
 
 
@@ -51,12 +52,11 @@ def tile_picked_selfkernfracunder_none_p_kernel(
                     nc.tensor.matmul(bank[:, cols], term[:, cols], ident[:], is_transpose=True,
                                      start=(i == 0), stop=(i == len(terms) - 1))
 
-        def flip_block(bank, b, terms_of_t):
+        def flip_pairs(bank, pairs_of_t):
             for t in range(4):
-                terms = terms_of_t[t]
-                for i, term in enumerate(terms):
-                    nc.tensor.matmul(bank[:, t * P:(t + 1) * P], term[:, b * P:(b + 1) * P], ident[:], is_transpose=True,
-                                     start=(i == 0), stop=(i == len(terms) - 1))
+                for i in range(2):
+                    nc.tensor.matmul(bank[:, t * P:(t + 1) * P], pairs_of_t[t][:, i, :], ident[:], is_transpose=True,
+                                     start=(i == 0), stop=(i == 1))
 
         xs = keep.tile([P, T], U8, name="xs")
         nc.gpsimd.memset(xs[:].bitcast(I32), 0)
@@ -111,69 +111,69 @@ def tile_picked_selfkernfracunder_none_p_kernel(
                 nc.scalar.activation(win[t][:, cols], acc[:, :width], ACT.Copy)
             nc.sync.dma_start(y_plain[t][:], win[t][:, :S])
 
-        neg = [[keep.tile([P, S], F32, name="neg%d_%d" % (t, i)) for i in range(2)] for t in range(4)]
-        kr = [[keep.tile([P, S], F32, name="kr%d_%d" % (t, i)) for i in range(2)] for t in range(4)]
+        neg = [keep.tile([P, 2, S], F32, name="neg%d" % t) for t in range(4)]
+        kr = [keep.tile([P, 4, 2, P], F32, name="kr%d" % t) for t in range(4)]
         for t in range(4):
             for i, lst in enumerate((l1, l2)):
-                nc.vector.tensor_scalar(neg[t][i][:], win[t][:].indirect(lst[:]), -1.0, 0.0, ALU.mult, ALU.add)
+                nc.vector.tensor_scalar(neg[t][:, i, :], win[t][:].indirect(lst[:]), -1.0, 0.0, ALU.mult, ALU.add)
                 if t == 3 and i == 1:
                     sq = keep.tile([P, S], F32, name="sq_last", tag="late")
                 else:
                     sq = ring.tile([P, S], F32, name="sq")
-                dealt = kr[t][i][:].rearrange("p (b g a) -> p b g a", b=4, a=8)
+                dealt = kr[t][:, :, i, :].rearrange("p b (g a) -> p b g a", a=8)
                 if PE_DIFF[t][i]:
                     diff = psum.tile([P, S], F32, name="diff", tag="diff")
-                    flip(diff, (neg[t][i], win[t]))
+                    flip(diff, (neg[t][:, i, :], win[t]))
                     nc.scalar.activation(sq[:], diff[:], ACT.Square)
                     back = psum.tile([P, S], F32, name="back", tag="back")
                     flip(back, (sq,))
                     src = back
                 else:
                     dv = ring.tile([P, S], F32, name="dv")
-                    nc.vector.tensor_tensor(dv[:], neg[t][i][:], win[t][:, :S], ALU.add)
+                    nc.vector.tensor_tensor(dv[:], neg[t][:, i, :], win[t][:, :S], ALU.add)
                     nc.scalar.activation(sq[:], dv[:], ACT.Square)
                     src = sq
                 nc.scalar.activation(dealt, src[:].rearrange("p (g b a) -> p b g a", b=4, a=8), ACT.Exp, scale=-0.5)
 
-        gap = keep.tile([P, 4, S], F32, name="gap")
+        d4 = [keep.tile([P, S], F32, name="d4_%d" % t) for t in range(4)]
         for t in range(4):
-            d4 = ring.tile([P, S], F32, name="d4")
-            nc.vector.tensor_tensor(d4[:], win[t][:].indirect(l4[:]), y_plain[t][:], ALU.subtract)
-            nc.scalar.activation(gap[:, t, :], d4[:], ACT.Abs)
+            nc.vector.tensor_tensor(d4[t][:], win[t][:].indirect(l4[:]), y_plain[t][:], ALU.subtract)
         d3 = [keep.tile([P, S], F32, name="d3_%d" % t) for t in range(4)]
         for t in range(4):
             nc.vector.tensor_tensor(d3[t][:], win[t][:].indirect(l3[:]), y_plain[t][:], ALU.subtract)
 
-        prod = [[keep.tile([P, S], F32, name="prod%d_%d" % (t, i)) for i in range(2)] for t in range(4)]
+        prod = [None] * 4
 
         def products(b):
+            prod[b] = keep.tile([P, 4, 2, P], F32, name="prod%d" % b, tag=("prod0", "d3_3", "inv0", "inv1")[b])
             for t in range(4):
-                for i in range(2):
-                    nc.vector.scalar_tensor_tensor(
-                        prod[t][i][:, b * P:(b + 1) * P].rearrange("p (g a) -> p g a", a=8),
-                        neg[t][i][:].rearrange("p (g b a) -> p b g a", b=4, a=8)[:, b],
-                        ga_t[t][:],
-                        kr[t][i][:, b * P:(b + 1) * P].rearrange("p (g a) -> p g a", a=8),
-                        ALU.mult, ALU.mult)
+                nc.vector.scalar_tensor_tensor(
+                    prod[b][:, t].rearrange("p i (g a) -> p (i g) a", a=8),
+                    neg[t][:].rearrange("p i (g b a) -> p b (i g) a", b=4, a=8)[:, b],
+                    ga_t[t][:],
+                    kr[t][:, b].rearrange("p i (g a) -> p (i g) a", a=8),
+                    ALU.mult, ALU.mult)
 
-        root2 = keep.tile([P, 4, S], F32, name="root2", tag="late")
+        gap = keep.tile([P, 4, S], F32, name="gap", tag="late")
         z2_planes = keep.tile([P, 4, S], BF16, name="z2_planes")
 
         def second_factor(t):
-            nc.scalar.activation(root2[:, t, :], gap[:, t, :], ACT.Abs_reciprocal_sqrt, bias=0.5)
-            inv2 = ring.tile([P, S], F32, name="inv2")
-            nc.scalar.activation(inv2[:], root2[:, t, :], ACT.Square)
+            nc.scalar.activation(gap[:, t, :], d4[t][:], ACT.Abs)
+            root2 = ring.tile([P, S], F32, name="root2")
+            nc.scalar.activation(root2[:], gap[:, t, :], ACT.Abs_reciprocal_sqrt, bias=0.5)
+            inv2 = ring.tile([P, S], F32, name="inv2", bufs=4)
+            nc.scalar.activation(inv2[:], root2[:], ACT.Square)
             nc.vector.scalar_tensor_tensor(z2_planes[:, t, :], d3[t][:], gb_t[t][:], inv2[:], ALU.mult, ALU.mult)
 
         inv = [None] * 4
 
         def inverse(b):
             den = psum.tile([P, S], F32, name="den", tag="diff")
-            flip_block(den, b, kr)
+            flip_pairs(den, [kr[t][:, b] for t in range(4)])
             root = ring.tile([P, S], F32, name="root")
             nc.scalar.activation(root[:].rearrange("q (u p e) -> q u p e", u=2, e=2),
                                  den[:].rearrange("q (u e p) -> q u p e", u=2, e=2), ACT.Abs_reciprocal_sqrt, bias=0.5)
-            inv[b] = ring.tile([P, S], F32, name="inv")
+            inv[b] = keep.tile([P, S], F32, name="inv%d" % b)
             nc.scalar.activation(inv[b][:], root[:], ACT.Square)
 
         z_c = [keep.tile([P, P], U32, name="z_c%d" % b, align_bytes=64) for b in range(4)]
@@ -182,7 +182,7 @@ def tile_picked_selfkernfracunder_none_p_kernel(
 
         def first_factor(b):
             num = psum.tile([P, S], F32, name="num", tag="back")
-            flip_block(num, b, prod)
+            flip_pairs(num, [prod[b][:, t] for t in range(4)])
             z_t = ring.tile([P, S], BF16, name="z_t")
             nc.vector.tensor_tensor(z_t[:].rearrange("q (u p e) -> q u p e", u=2, e=2),
                                     num[:].rearrange("q (u e p) -> q u p e", u=2, e=2),

@@ -18,8 +18,10 @@ T = 2048
 S = 512
 WINDOW = 1024
 FLOPS = 2 * 2 * 512 * 512 * 512
-PROD_BUFS = 1
-PE_DIFF = ((True, True), (True, True), (True, True), (True, True))
+OFFLOAD = (0,)
+GAP_TAG = "sq0"
+ROOT_TAG = "sq1"
+PE_DIFF = ((True, False), (True, True), (True, False), (True, True))
 
 
 def tile_picked_selfkernfracunder_none_p_kernel(
@@ -29,7 +31,7 @@ def tile_picked_selfkernfracunder_none_p_kernel(
     with ExitStack() as ctx:
         keep = ctx.enter_context(tc.tile_pool(name="keep", bufs=1))
         ring = ctx.enter_context(tc.tile_pool(name="ring", bufs=2))
-        psum = ctx.enter_context(tc.psum_pool(name="psum", bufs=2))
+        psum = ctx.enter_context(tc.psum_pool(name="psum", bufs=1))
 
         def load_list(name, src):
             tile = keep.tile([P, S // 16], U16, name=name)
@@ -105,7 +107,7 @@ def tile_picked_selfkernfracunder_none_p_kernel(
             width = 256 if t == 0 else S
             for c0 in range(0, S, width):
                 cols = slice(c0, c0 + width)
-                acc = psum.tile([P, S], F32, name="acc", tag="acc")
+                acc = psum.tile([P, S], F32, name="acc", tag="bank%d" % ((t + c0 // 256) % 2 if t == 0 else (t + 1) % 2))
                 nc.tensor.matmul_mx(out=acc[:, :width], lhsT=w_c[t][:].bitcast(FP8X4), lhsT_scale=w_s[t][:],
                                     rhs=xq[:, cols].bitcast(FP8X4), rhs_scale=xq_s[:, cols], start=True, stop=True)
                 nc.scalar.activation(win[t][:, cols], acc[:, :width], ACT.Copy)
@@ -113,23 +115,22 @@ def tile_picked_selfkernfracunder_none_p_kernel(
 
         neg = [keep.tile([P, 2, S], F32, name="neg%d" % t) for t in range(4)]
         kr = [keep.tile([P, 4, 2, P], F32, name="kr%d" % t) for t in range(4)]
+        turn = 0
         for t in range(4):
             for i, lst in enumerate((l1, l2)):
                 nc.vector.tensor_scalar(neg[t][:, i, :], win[t][:].indirect(lst[:]), -1.0, 0.0, ALU.mult, ALU.add)
-                if t == 3 and i == 1:
-                    sq = keep.tile([P, S], F32, name="sq_last", tag="late")
-                else:
-                    sq = ring.tile([P, S], F32, name="sq")
+                sq = keep.tile([P, S], F32, name="sq%d_%d" % (t, i), tag="sq%d" % i)
                 dealt = kr[t][:, :, i, :].rearrange("p b (g a) -> p b g a", a=8)
                 if PE_DIFF[t][i]:
-                    diff = psum.tile([P, S], F32, name="diff", tag="diff")
+                    diff = psum.tile([P, S], F32, name="diff", tag="bank%d" % (2 + turn % 2))
                     flip(diff, (neg[t][:, i, :], win[t]))
                     nc.scalar.activation(sq[:], diff[:], ACT.Square)
-                    back = psum.tile([P, S], F32, name="back", tag="back")
+                    back = psum.tile([P, S], F32, name="back", tag="bank%d" % (4 + turn % 2))
                     flip(back, (sq,))
                     src = back
+                    turn = turn + 1
                 else:
-                    dv = ring.tile([P, S], F32, name="dv")
+                    dv = keep.tile([P, S], F32, name="dv%d_%d" % (t, i))
                     nc.vector.tensor_tensor(dv[:], neg[t][:, i, :], win[t][:, :S], ALU.add)
                     nc.scalar.activation(sq[:], dv[:], ACT.Square)
                     src = sq
@@ -154,21 +155,21 @@ def tile_picked_selfkernfracunder_none_p_kernel(
                     kr[t][:, b].rearrange("p i (g a) -> p (i g) a", a=8),
                     ALU.mult, ALU.mult)
 
-        gap = keep.tile([P, 4, S], F32, name="gap", tag="late")
+        gap = keep.tile([P, 4, S], F32, name="gap", tag=GAP_TAG)
+        root2 = keep.tile([P, 4, S], F32, name="root2", tag=ROOT_TAG)
         z2_planes = keep.tile([P, 4, S], BF16, name="z2_planes")
 
         def second_factor(t):
             nc.scalar.activation(gap[:, t, :], d4[t][:], ACT.Abs)
-            root2 = ring.tile([P, S], F32, name="root2")
-            nc.scalar.activation(root2[:], gap[:, t, :], ACT.Abs_reciprocal_sqrt, bias=0.5)
+            nc.scalar.activation(root2[:, t, :], gap[:, t, :], ACT.Abs_reciprocal_sqrt, bias=0.5)
             inv2 = ring.tile([P, S], F32, name="inv2", bufs=4)
-            nc.scalar.activation(inv2[:], root2[:], ACT.Square)
+            nc.scalar.activation(inv2[:], root2[:, t, :], ACT.Square)
             nc.vector.scalar_tensor_tensor(z2_planes[:, t, :], d3[t][:], gb_t[t][:], inv2[:], ALU.mult, ALU.mult)
 
         inv = [None] * 4
 
         def inverse(b):
-            den = psum.tile([P, S], F32, name="den", tag="diff")
+            den = psum.tile([P, S], F32, name="den", tag="bank%d" % (2 + b))
             flip_pairs(den, [kr[t][:, b] for t in range(4)])
             root = ring.tile([P, S], F32, name="root")
             nc.scalar.activation(root[:].rearrange("q (u p e) -> q u p e", u=2, e=2),
@@ -181,13 +182,13 @@ def tile_picked_selfkernfracunder_none_p_kernel(
         z_g = [None] * 4
 
         def first_factor(b):
-            num = psum.tile([P, S], F32, name="num", tag="back")
+            num = psum.tile([P, S], F32, name="num", tag="bank%d" % (2 + b))
             flip_pairs(num, [prod[b][:, t] for t in range(4)])
             z_t = ring.tile([P, S], BF16, name="z_t")
             nc.vector.tensor_tensor(z_t[:].rearrange("q (u p e) -> q u p e", u=2, e=2),
                                     num[:].rearrange("q (u e p) -> q u p e", u=2, e=2),
                                     inv[b][:].rearrange("q (u p e) -> q u p e", u=2, e=2), ALU.mult)
-            pairs = psum.tile([P, S], F32, name="pairs", tag="pairs")
+            pairs = psum.tile([P, S], F32, name="pairs", tag="bank%d" % (6 + b % 2))
             words = z_t[:].bitcast(F32)
             for u in range(2):
                 nc.tensor.transpose(pairs[:, u * P:(u + 1) * P], words[:, u * P:(u + 1) * P], ident[:])
@@ -222,42 +223,54 @@ def tile_picked_selfkernfracunder_none_p_kernel(
         out_rows = out.rearrange("(g b a) n -> b g a n", b=4, a=8)
 
         def second_product(b):
-            acc = psum.tile([P, S], F32, name="acc2", tag="acc")
+            acc = psum.tile([P, S], F32, name="acc2", tag="bank%d" % (b % 2))
             nc.tensor.matmul_mx(out=acc[:], lhsT=z_c[b][:].bitcast(FP8X4), lhsT_scale=z_s[b][:],
                                 rhs=z2_c[:].bitcast(FP8X4), rhs_scale=z2_s[:], start=True, stop=True)
+            if b in OFFLOAD:
+                nc.scalar.activation(win[b][:, :S], acc[:], ACT.Copy, scale=0.0625)
+                return
             nc.scalar.activation(win[b][:, :S], acc[:], ACT.Copy, scale=-0.0625)
-            s_plain[b] = ring.tile([P, S], F32, name="s_plain")
+            s_plain[b] = ring.tile([P, S], F32, name="s_plain", bufs=4)
             nc.scalar.activation(s_plain[b][:], acc[:], ACT.Copy, scale=0.0625)
 
         def finish(b, pieces):
+            if b in OFFLOAD:
+                g5 = ring.tile([P, S], F32, name="f5", bufs=5)
+                nc.vector.tensor_scalar(g5[:], win[b][:].indirect(l5[:]), -1.0, 0.0, ALU.mult, ALU.add)
+                step = ring.tile([P, S], F32, name="f6", bufs=5)
+                nc.vector.tensor_tensor(step[:], win[b][:].indirect(l6[:]), g5[:], ALU.add)
+                over = ring.tile([P, S], F32, name="over")
+                nc.scalar.activation(over[:], step[:], ACT.Relu, scale=-1.0)
+                total = psum.tile([P, S], F32, name="total", tag="bank%d" % (2 + b))
+                flip(total, (win[b], g5, over))
+                turned = ring.tile([P, S], F32, name="turned")
+                nc.scalar.activation(turned[:], total[:], ACT.Copy)
+                home = psum.tile([P, S], F32, name="home", tag="bank%d" % (6 + b % 2))
+                flip(home, (turned,))
+                res = ring.tile([P, S], F32, name="res", bufs=5)
+                nc.scalar.activation(res[:], home[:], ACT.Copy)
+                nc.scalar.dma_start(out_rows[b], res[:])
+                return
             width = S // pieces
             for h in range(pieces):
                 cols = slice(h * width, (h + 1) * width)
                 lcols = slice(h * width // 16, (h + 1) * width // 16)
-                f5 = ring.tile([P, width], F32, name="f5")
-                f6 = ring.tile([P, width], F32, name="f6")
-                res = ring.tile([P, width], F32, name="res", bufs=3)
+                f5 = ring.tile([P, width], F32, name="f5", bufs=5)
+                f6 = ring.tile([P, width], F32, name="f6", bufs=5)
+                res = ring.tile([P, width], F32, name="res", bufs=5)
                 nc.vector.tensor_tensor(f5[:], win[b][:].indirect(l5[:, lcols]), s_plain[b][:, cols], ALU.add)
                 nc.vector.tensor_tensor(f6[:], win[b][:].indirect(l6[:, lcols]), s_plain[b][:, cols], ALU.add)
                 nc.vector.tensor_tensor(res[:], f5[:], f6[:], ALU.max)
                 nc.sync.dma_start(out_rows[b][:, :, cols], res[:])
 
         second_product(0)
-        inverse(1)
-        first_factor(1)
-        products(2)
-        quantise_first(1)
-        second_product(1)
-        inverse(2)
-        finish(0, 1)
-        first_factor(2)
-        products(3)
-        quantise_first(2)
-        second_product(2)
-        inverse(3)
-        finish(1, 1)
-        first_factor(3)
-        quantise_first(3)
-        second_product(3)
-        finish(2, 1)
+        for b in range(1, 4):
+            inverse(b)
+            first_factor(b)
+            if b < 3:
+                products(b + 1)
+            quantise_first(b)
+            second_product(b)
+        for b in range(3):
+            finish(b, 1)
         finish(3, 2)

@@ -16,12 +16,17 @@ ACT = mybir.ActivationFunctionType
 P = 128
 T = 2048
 S = 512
-WINDOW = 1024
+HALF = S // 2
+TILES = 4
+RUN = 8
+WINDOW = 2 * S
 FLOPS = 2 * 2 * 512 * 512 * 512
-OFFLOAD = (0,)
-GAP_TAG = "sq0"
-ROOT_TAG = "sq1"
-PE_DIFF = ((True, False), (True, True), (True, False), (True, True))
+
+VECTOR_DIFFERENCE = (1, 1)
+TURNED_BLOCKS = 2
+VECTOR_CASTS = 2
+
+PRODUCT_BANK, MIDDLE_BANK, RETURN_BANK = 0, 2, 6
 
 
 def tile_picked_selfkernfracunder_none_p_kernel(
@@ -33,42 +38,45 @@ def tile_picked_selfkernfracunder_none_p_kernel(
         ring = ctx.enter_context(tc.tile_pool(name="ring", bufs=2))
         psum = ctx.enter_context(tc.psum_pool(name="psum", bufs=1))
 
+        def bank(name, number):
+            return psum.tile([P, S], F32, name=name, tag="bank%d" % number)
+
         def load_list(name, src):
             tile = keep.tile([P, S // 16], U16, name=name)
             nc.sync.dma_start(tile[:], src)
             return tile
 
         def load_gain(name, src):
-            cols = []
-            for t in range(4):
-                col = keep.tile([P, 1], F32, name="%s%d" % (name, t))
+            columns = []
+            for t in range(TILES):
+                column = keep.tile([P, 1], F32, name="%s%d" % (name, t))
                 with nc.allow_non_contiguous_dma(reason="one value a partition"):
-                    nc.sync.dma_start(col[:], src.rearrange("(g t a) o -> t g a o", t=4, a=8)[t])
-                cols.append(col)
-            return cols
+                    nc.sync.dma_start(column[:], src.rearrange("(g t a) o -> t g a o", t=TILES, a=RUN)[t])
+                columns.append(column)
+            return columns
 
-        def flip(bank, terms):
-            for c in range(4):
-                cols = slice(c * P, (c + 1) * P)
-                for i, term in enumerate(terms):
-                    nc.tensor.matmul(bank[:, cols], term[:, cols], ident[:], is_transpose=True,
-                                     start=(i == 0), stop=(i == len(terms) - 1))
+        def turn_sum(dst, terms_of_block):
+            for c, terms in enumerate(terms_of_block):
+                for place, term in enumerate(terms):
+                    nc.tensor.matmul(dst[:, c * P:(c + 1) * P], term, ident[:], is_transpose=True,
+                                     start=(place == 0), stop=(place == len(terms) - 1))
 
-        def flip_pairs(bank, pairs_of_t):
-            for t in range(4):
-                for i in range(2):
-                    nc.tensor.matmul(bank[:, t * P:(t + 1) * P], pairs_of_t[t][:, i, :], ident[:], is_transpose=True,
-                                     start=(i == 0), stop=(i == 1))
+        def blocks_of(*tiles):
+            return [[tile[:, c * P:(c + 1) * P] for tile in tiles] for c in range(TILES)]
 
-        xs = keep.tile([P, T], U8, name="xs")
-        nc.gpsimd.memset(xs[:].bitcast(I32), 0)
+        def pairs_of(tiles):
+            return [[tile[:, i, :] for i in range(2)] for tile in tiles]
+
+        x_scale_rows = keep.tile([P, T], U8, name="x_scale_rows")
+        nc.gpsimd.memset(x_scale_rows[:].bitcast(I32), 0)
         l_offs = load_list("l_offs", offs)
-        for q in range(4):
-            nc.sync.dma_start(xs[32 * q:32 * q + 4, :].bitcast(I32), x_scales[0, 4 * q:4 * q + 4, :].bitcast(I32))
+        for quad in range(4):
+            nc.sync.dma_start(x_scale_rows[32 * quad:32 * quad + 4, :].bitcast(I32),
+                              x_scales[0, 4 * quad:4 * quad + 4, :].bitcast(I32))
         w_raw = keep.tile([P, 4, S], F32, name="w_raw")
         nc.sync.dma_start(w_raw[:], w1.rearrange("(p j) c -> p j c", j=4))
-        xw = keep.tile([P, T], I32, name="xw")
-        nc.sync.dma_start(xw[:], x_words[0].rearrange("p n t -> p (n t)").bitcast(I32))
+        x_table = keep.tile([P, T], I32, name="x_table")
+        nc.sync.dma_start(x_table[:], x_words[0].rearrange("p token j -> p (token j)").bitcast(I32))
         l1 = load_list("l1", n1)
         l2 = load_list("l2", n2)
         l4 = load_list("l4", n4)
@@ -80,197 +88,194 @@ def tile_picked_selfkernfracunder_none_p_kernel(
 
         ident = keep.tile([P, P], F32, name="ident")
         make_identity(nc, ident[:])
-        win = [keep.tile([P, WINDOW], F32, name="win%d" % t) for t in range(4)]
-        for t in range(4):
-            nc.vector.memset(win[t][:, S:], 0.0)
+        window = [keep.tile([P, WINDOW], F32, name="window%d" % t) for t in range(TILES)]
+        for t in range(TILES):
+            nc.vector.memset(window[t][:, S:], 0.0)
 
-        xq_s = keep.tile([P, S], U8, name="xq_s", align_bytes=64)
-        nc.vector.tensor_copy(xq_s[:], xs[:].indirect(l_offs[:]))
+        x_s = keep.tile([P, S], U8, name="x_s", align_bytes=64)
+        nc.vector.tensor_copy(x_s[:], x_scale_rows[:].indirect(l_offs[:]))
         w_c, w_s = [], []
-        w_view = w_raw[:].rearrange("p j (g t a) -> p t g a j", t=4, a=8)
-        for t in range(4):
-            wg = keep.tile([P, S], BF16, name="wg%d" % t, align_bytes=64)
-            dst = wg[:].rearrange("p (g a j) -> p g a j", a=8, j=4)
-            if t < 2:
-                nc.vector.tensor_copy(dst, w_view[:, t])
+        w_dealt = w_raw[:].rearrange("p j (g t a) -> p t g a j", t=TILES, a=RUN)
+        for t in range(TILES):
+            w_bf = keep.tile([P, S], BF16, name="w_bf%d" % t, align_bytes=64)
+            w_bf_view = w_bf[:].rearrange("p (g a j) -> p g a j", a=RUN, j=4)
+            if t < VECTOR_CASTS:
+                nc.vector.tensor_copy(w_bf_view, w_dealt[:, t])
             else:
-                nc.scalar.activation(dst, w_view[:, t], ACT.Copy)
+                nc.scalar.activation(w_bf_view, w_dealt[:, t], ACT.Copy)
             w_c.append(keep.tile([P, P], U32, name="w_c%d" % t, align_bytes=64))
             w_s.append(keep.tile([P, P], U8, name="w_s%d" % t, align_bytes=64))
-            nc.vector.quantize_mx(out=w_c[t][:].bitcast(FP8X4), scales=w_s[t][:], in_=wg[:])
-        xq = keep.tile([P, S], U32, name="xq", align_bytes=64)
+            nc.vector.quantize_mx(out=w_c[t][:].bitcast(FP8X4), scales=w_s[t][:], in_=w_bf[:])
+        x_c = keep.tile([P, S], U32, name="x_c", align_bytes=64)
         for h in range(2):
-            nc.vector.tensor_copy(xq[:, h * 256:(h + 1) * 256], xw[:].bitcast(U32).indirect(l_offs[:, h * 16:(h + 1) * 16]))
+            nc.vector.tensor_copy(x_c[:, h * HALF:(h + 1) * HALF],
+                                  x_table[:].bitcast(U32).indirect(l_offs[:, h * HALF // 16:(h + 1) * HALF // 16]))
 
-        y_plain = [keep.tile([P, S], F32, name="y_plain%d" % t) for t in range(4)]
-        for t in range(4):
-            width = 256 if t == 0 else S
-            for c0 in range(0, S, width):
-                cols = slice(c0, c0 + width)
-                acc = psum.tile([P, S], F32, name="acc", tag="bank%d" % ((t + c0 // 256) % 2 if t == 0 else (t + 1) % 2))
-                nc.tensor.matmul_mx(out=acc[:, :width], lhsT=w_c[t][:].bitcast(FP8X4), lhsT_scale=w_s[t][:],
-                                    rhs=xq[:, cols].bitcast(FP8X4), rhs_scale=xq_s[:, cols], start=True, stop=True)
-                nc.scalar.activation(win[t][:, cols], acc[:, :width], ACT.Copy)
-            nc.sync.dma_start(y_plain[t][:], win[t][:, :S])
+        y_plain = [keep.tile([P, S], F32, name="y_plain%d" % t) for t in range(TILES)]
+        passes = [(0, 0, HALF), (0, HALF, S)] + [(t, 0, S) for t in range(1, TILES)]
+        for number, (t, c0, c1) in enumerate(passes):
+            acc = bank("y_acc", PRODUCT_BANK + number % 2)
+            nc.tensor.matmul_mx(out=acc[:, :c1 - c0], lhsT=w_c[t][:].bitcast(FP8X4), lhsT_scale=w_s[t][:],
+                                rhs=x_c[:, c0:c1].bitcast(FP8X4), rhs_scale=x_s[:, c0:c1], start=True, stop=True)
+            nc.scalar.activation(window[t][:, c0:c1], acc[:, :c1 - c0], ACT.Copy)
+            if c1 == S:
+                nc.sync.dma_start(y_plain[t][:], window[t][:, :S])
 
-        neg = [keep.tile([P, 2, S], F32, name="neg%d" % t) for t in range(4)]
-        kr = [keep.tile([P, 4, 2, P], F32, name="kr%d" % t) for t in range(4)]
-        turn = 0
-        for t in range(4):
+        neg = [keep.tile([P, 2, S], F32, name="neg%d" % t) for t in range(TILES)]
+        kr = [keep.tile([P, TILES, 2, P], F32, name="kr%d" % t) for t in range(TILES)]
+        turns = 0
+        for t in range(TILES):
             for i, lst in enumerate((l1, l2)):
-                nc.vector.tensor_scalar(neg[t][:, i, :], win[t][:].indirect(lst[:]), -1.0, 0.0, ALU.mult, ALU.add)
-                sq = keep.tile([P, S], F32, name="sq%d_%d" % (t, i), tag="sq%d" % i)
-                dealt = kr[t][:, :, i, :].rearrange("p b (g a) -> p b g a", a=8)
-                if PE_DIFF[t][i]:
-                    diff = psum.tile([P, S], F32, name="diff", tag="bank%d" % (2 + turn % 2))
-                    flip(diff, (neg[t][:, i, :], win[t]))
-                    nc.scalar.activation(sq[:], diff[:], ACT.Square)
-                    back = psum.tile([P, S], F32, name="back", tag="bank%d" % (4 + turn % 2))
-                    flip(back, (sq,))
-                    src = back
-                    turn = turn + 1
+                nc.vector.tensor_scalar(neg[t][:, i, :], window[t][:].indirect(lst[:]), -1.0, 0.0, ALU.mult, ALU.add)
+                square = keep.tile([P, S], F32, name="square%d_%d" % (t, i), tag="square%d" % i)
+                if (t, i) == VECTOR_DIFFERENCE:
+                    diff = keep.tile([P, S], F32, name="diff")
+                    nc.vector.tensor_tensor(diff[:], neg[t][:, i, :], window[t][:, :S], ALU.add)
+                    nc.scalar.activation(square[:], diff[:], ACT.Square)
+                    upright = square
                 else:
-                    dv = keep.tile([P, S], F32, name="dv%d_%d" % (t, i))
-                    nc.vector.tensor_tensor(dv[:], neg[t][:, i, :], win[t][:, :S], ALU.add)
-                    nc.scalar.activation(sq[:], dv[:], ACT.Square)
-                    src = sq
-                nc.scalar.activation(dealt, src[:].rearrange("p (g b a) -> p b g a", b=4, a=8), ACT.Exp, scale=-0.5)
+                    diff_turned = bank("diff_turned", MIDDLE_BANK + turns % 2)
+                    turn_sum(diff_turned, blocks_of(neg[t][:, i, :], window[t]))
+                    nc.scalar.activation(square[:], diff_turned[:], ACT.Square)
+                    upright = bank("square_upright", MIDDLE_BANK + 2 + turns % 2)
+                    turn_sum(upright, blocks_of(square))
+                    turns = turns + 1
+                nc.scalar.activation(kr[t][:, :, i, :].rearrange("p b (g a) -> p b g a", a=RUN),
+                                     upright[:].rearrange("p (g b a) -> p b g a", b=TILES, a=RUN), ACT.Exp, scale=-0.5)
 
-        d4 = [keep.tile([P, S], F32, name="d4_%d" % t) for t in range(4)]
-        for t in range(4):
-            nc.vector.tensor_tensor(d4[t][:], win[t][:].indirect(l4[:]), y_plain[t][:], ALU.subtract)
-        d3 = [keep.tile([P, S], F32, name="d3_%d" % t) for t in range(4)]
-        for t in range(4):
-            nc.vector.tensor_tensor(d3[t][:], win[t][:].indirect(l3[:]), y_plain[t][:], ALU.subtract)
+        d4 = [keep.tile([P, S], F32, name="d4_%d" % t) for t in range(TILES)]
+        for t in range(TILES):
+            nc.vector.tensor_tensor(d4[t][:], window[t][:].indirect(l4[:]), y_plain[t][:], ALU.subtract)
+        d3 = [keep.tile([P, S], F32, name="d3_%d" % t) for t in range(TILES)]
+        for t in range(TILES):
+            nc.vector.tensor_tensor(d3[t][:], window[t][:].indirect(l3[:]), y_plain[t][:], ALU.subtract)
 
-        prod = [None] * 4
+        weighted_tags = ("weighted0", "d3_%d" % (TILES - 1), "inverse0", "inverse1")
+        weighted = [None] * TILES
 
-        def products(b):
-            prod[b] = keep.tile([P, 4, 2, P], F32, name="prod%d" % b, tag=("prod0", "d3_3", "inv0", "inv1")[b])
-            for t in range(4):
+        def weigh(b):
+            weighted[b] = keep.tile([P, TILES, 2, P], F32, name="weighted%d" % b, tag=weighted_tags[b])
+            for t in range(TILES):
                 nc.vector.scalar_tensor_tensor(
-                    prod[b][:, t].rearrange("p i (g a) -> p (i g) a", a=8),
-                    neg[t][:].rearrange("p i (g b a) -> p b (i g) a", b=4, a=8)[:, b],
+                    weighted[b][:, t].rearrange("p i (g a) -> p (i g) a", a=RUN),
+                    neg[t][:].rearrange("p i (g b a) -> p b (i g) a", b=TILES, a=RUN)[:, b],
                     ga_t[t][:],
-                    kr[t][:, b].rearrange("p i (g a) -> p (i g) a", a=8),
+                    kr[t][:, b].rearrange("p i (g a) -> p (i g) a", a=RUN),
                     ALU.mult, ALU.mult)
 
-        gap = keep.tile([P, 4, S], F32, name="gap", tag=GAP_TAG)
-        root2 = keep.tile([P, 4, S], F32, name="root2", tag=ROOT_TAG)
-        z2_planes = keep.tile([P, 4, S], BF16, name="z2_planes")
+        gap = keep.tile([P, TILES, S], F32, name="gap", tag="square0")
+        gap_root = keep.tile([P, TILES, S], F32, name="gap_root", tag="square1")
+        z2_planes = keep.tile([P, TILES, S], BF16, name="z2_planes")
 
         def second_factor(t):
             nc.scalar.activation(gap[:, t, :], d4[t][:], ACT.Abs)
-            nc.scalar.activation(root2[:, t, :], gap[:, t, :], ACT.Abs_reciprocal_sqrt, bias=0.5)
-            inv2 = ring.tile([P, S], F32, name="inv2", bufs=4)
-            nc.scalar.activation(inv2[:], root2[:, t, :], ACT.Square)
-            nc.vector.scalar_tensor_tensor(z2_planes[:, t, :], d3[t][:], gb_t[t][:], inv2[:], ALU.mult, ALU.mult)
+            nc.scalar.activation(gap_root[:, t, :], gap[:, t, :], ACT.Abs_reciprocal_sqrt, bias=0.5)
+            gap_inverse = ring.tile([P, S], F32, name="gap_inverse", bufs=TILES)
+            nc.scalar.activation(gap_inverse[:], gap_root[:, t, :], ACT.Square)
+            nc.vector.scalar_tensor_tensor(z2_planes[:, t, :], d3[t][:], gb_t[t][:], gap_inverse[:], ALU.mult, ALU.mult)
 
-        inv = [None] * 4
+        inverse = [None] * TILES
 
-        def inverse(b):
-            den = psum.tile([P, S], F32, name="den", tag="bank%d" % (2 + b))
-            flip_pairs(den, [kr[t][:, b] for t in range(4)])
-            root = ring.tile([P, S], F32, name="root")
-            nc.scalar.activation(root[:].rearrange("q (u p e) -> q u p e", u=2, e=2),
+        def invert(b):
+            den = bank("den", MIDDLE_BANK + b)
+            turn_sum(den, pairs_of([kr[t][:, b] for t in range(TILES)]))
+            den_root = ring.tile([P, S], F32, name="den_root")
+            nc.scalar.activation(den_root[:].rearrange("q (u p e) -> q u p e", u=2, e=2),
                                  den[:].rearrange("q (u e p) -> q u p e", u=2, e=2), ACT.Abs_reciprocal_sqrt, bias=0.5)
-            inv[b] = keep.tile([P, S], F32, name="inv%d" % b)
-            nc.scalar.activation(inv[b][:], root[:], ACT.Square)
+            inverse[b] = keep.tile([P, S], F32, name="inverse%d" % b)
+            nc.scalar.activation(inverse[b][:], den_root[:], ACT.Square)
 
-        z_c = [keep.tile([P, P], U32, name="z_c%d" % b, align_bytes=64) for b in range(4)]
-        z_s = [keep.tile([P, P], U8, name="z_s%d" % b, align_bytes=64) for b in range(4)]
-        z_g = [None] * 4
+        z_c = [keep.tile([P, P], U32, name="z_c%d" % b, align_bytes=64) for b in range(TILES)]
+        z_s = [keep.tile([P, P], U8, name="z_s%d" % b, align_bytes=64) for b in range(TILES)]
+        z_bf = [None] * TILES
 
         def first_factor(b):
-            num = psum.tile([P, S], F32, name="num", tag="bank%d" % (2 + b))
-            flip_pairs(num, [prod[b][:, t] for t in range(4)])
-            z_t = ring.tile([P, S], BF16, name="z_t")
-            nc.vector.tensor_tensor(z_t[:].rearrange("q (u p e) -> q u p e", u=2, e=2),
+            num = bank("num", MIDDLE_BANK + b)
+            turn_sum(num, pairs_of([weighted[b][:, t] for t in range(TILES)]))
+            z_turned = ring.tile([P, S], BF16, name="z_turned")
+            nc.vector.tensor_tensor(z_turned[:].rearrange("q (u p e) -> q u p e", u=2, e=2),
                                     num[:].rearrange("q (u e p) -> q u p e", u=2, e=2),
-                                    inv[b][:].rearrange("q (u p e) -> q u p e", u=2, e=2), ALU.mult)
-            pairs = psum.tile([P, S], F32, name="pairs", tag="bank%d" % (6 + b % 2))
-            words = z_t[:].bitcast(F32)
+                                    inverse[b][:].rearrange("q (u p e) -> q u p e", u=2, e=2), ALU.mult)
+            z_words = bank("z_words", RETURN_BANK + b % 2)
             for u in range(2):
-                nc.tensor.transpose(pairs[:, u * P:(u + 1) * P], words[:, u * P:(u + 1) * P], ident[:])
-            z_g[b] = ring.tile([P, S], BF16, name="z_g", align_bytes=64)
-            nc.scalar.copy(z_g[b][:].bitcast(F32).rearrange("p (j u) -> p j u", u=2),
-                           pairs[:, :2 * P].rearrange("p (u j) -> p j u", u=2))
+                nc.tensor.transpose(z_words[:, u * P:(u + 1) * P], z_turned[:].bitcast(F32)[:, u * P:(u + 1) * P], ident[:])
+            z_bf[b] = ring.tile([P, S], BF16, name="z_bf", align_bytes=64)
+            nc.scalar.copy(z_bf[b][:].bitcast(F32).rearrange("p (q u) -> p q u", u=2),
+                           z_words[:, :2 * P].rearrange("p (u q) -> p q u", u=2))
 
         def quantise_first(b):
-            nc.vector.quantize_mx(out=z_c[b][:].bitcast(FP8X4), scales=z_s[b][:], in_=z_g[b][:])
+            nc.vector.quantize_mx(out=z_c[b][:].bitcast(FP8X4), scales=z_s[b][:], in_=z_bf[b][:])
 
-        products(0)
-        second_factor(0)
-        second_factor(1)
-        second_factor(2)
-        second_factor(3)
-        inverse(0)
-        z2_g = keep.tile([P, S * 4], BF16, name="z2_g", align_bytes=64)
+        weigh(0)
+        for t in range(TILES):
+            second_factor(t)
+        invert(0)
+        z2_bf = keep.tile([P, S * TILES], BF16, name="z2_bf", align_bytes=64)
         z2_c = keep.tile([P, S], U32, name="z2_c", align_bytes=64)
         z2_s = keep.tile([P, S], U8, name="z2_s", align_bytes=64)
         first_factor(0)
         for h in range(2):
             nc.scalar.copy(
-                z2_g[:, h * 1024:(h + 1) * 1024].rearrange("p (c i t) -> p c t i", i=4, t=4),
-                z2_planes[:, :, h * 256:(h + 1) * 256].rearrange("p t (c i) -> p c t i", i=4))
-        products(1)
+                z2_bf[:, h * HALF * TILES:(h + 1) * HALF * TILES].rearrange("p (c near t) -> p c t near", near=4, t=TILES),
+                z2_planes[:, :, h * HALF:(h + 1) * HALF].rearrange("p t (c near) -> p c t near", near=4))
+        weigh(1)
         quantise_first(0)
         for h in range(2):
-            nc.vector.quantize_mx(out=z2_c[:, h * 256:(h + 1) * 256].bitcast(FP8X4), scales=z2_s[:, h * 256:(h + 1) * 256],
-                                  in_=z2_g[:, h * 1024:(h + 1) * 1024])
+            nc.vector.quantize_mx(out=z2_c[:, h * HALF:(h + 1) * HALF].bitcast(FP8X4), scales=z2_s[:, h * HALF:(h + 1) * HALF],
+                                  in_=z2_bf[:, h * HALF * TILES:(h + 1) * HALF * TILES])
 
-        s_plain = [None] * 4
-        out_rows = out.rearrange("(g b a) n -> b g a n", b=4, a=8)
+        s_plain = [None] * TILES
+        out_rows = out.rearrange("(g b a) column -> b g a column", b=TILES, a=RUN)
+        last_steps = TILES + 1
 
         def second_product(b):
-            acc = psum.tile([P, S], F32, name="acc2", tag="bank%d" % (b % 2))
+            acc = bank("s_acc", PRODUCT_BANK + b % 2)
             nc.tensor.matmul_mx(out=acc[:], lhsT=z_c[b][:].bitcast(FP8X4), lhsT_scale=z_s[b][:],
                                 rhs=z2_c[:].bitcast(FP8X4), rhs_scale=z2_s[:], start=True, stop=True)
-            if b in OFFLOAD:
-                nc.scalar.activation(win[b][:, :S], acc[:], ACT.Copy, scale=0.0625)
-                return
-            nc.scalar.activation(win[b][:, :S], acc[:], ACT.Copy, scale=-0.0625)
-            s_plain[b] = ring.tile([P, S], F32, name="s_plain", bufs=4)
-            nc.scalar.activation(s_plain[b][:], acc[:], ACT.Copy, scale=0.0625)
+            if b < TURNED_BLOCKS:
+                nc.scalar.activation(window[b][:, :S], acc[:], ACT.Copy, scale=0.0625)
+            else:
+                nc.scalar.activation(window[b][:, :S], acc[:], ACT.Copy, scale=-0.0625)
+                s_plain[b] = ring.tile([P, S], F32, name="s_plain", bufs=TILES)
+                nc.scalar.activation(s_plain[b][:], acc[:], ACT.Copy, scale=0.0625)
 
-        def finish(b, pieces):
-            if b in OFFLOAD:
-                g5 = ring.tile([P, S], F32, name="f5", bufs=5)
-                nc.vector.tensor_scalar(g5[:], win[b][:].indirect(l5[:]), -1.0, 0.0, ALU.mult, ALU.add)
-                step = ring.tile([P, S], F32, name="f6", bufs=5)
-                nc.vector.tensor_tensor(step[:], win[b][:].indirect(l6[:]), g5[:], ALU.add)
-                over = ring.tile([P, S], F32, name="over")
-                nc.scalar.activation(over[:], step[:], ACT.Relu, scale=-1.0)
-                total = psum.tile([P, S], F32, name="total", tag="bank%d" % (2 + b))
-                flip(total, (win[b], g5, over))
-                turned = ring.tile([P, S], F32, name="turned")
-                nc.scalar.activation(turned[:], total[:], ACT.Copy)
-                home = psum.tile([P, S], F32, name="home", tag="bank%d" % (6 + b % 2))
-                flip(home, (turned,))
-                res = ring.tile([P, S], F32, name="res", bufs=5)
-                nc.scalar.activation(res[:], home[:], ACT.Copy)
-                nc.scalar.dma_start(out_rows[b], res[:])
-                return
-            width = S // pieces
-            for h in range(pieces):
-                cols = slice(h * width, (h + 1) * width)
-                lcols = slice(h * width // 16, (h + 1) * width // 16)
-                f5 = ring.tile([P, width], F32, name="f5", bufs=5)
-                f6 = ring.tile([P, width], F32, name="f6", bufs=5)
-                res = ring.tile([P, width], F32, name="res", bufs=5)
-                nc.vector.tensor_tensor(f5[:], win[b][:].indirect(l5[:, lcols]), s_plain[b][:, cols], ALU.add)
-                nc.vector.tensor_tensor(f6[:], win[b][:].indirect(l6[:, lcols]), s_plain[b][:, cols], ALU.add)
-                nc.vector.tensor_tensor(res[:], f5[:], f6[:], ALU.max)
-                nc.sync.dma_start(out_rows[b][:, :, cols], res[:])
+        def finish_turned(b):
+            by_n5 = ring.tile([P, S], F32, name="by_n5", bufs=last_steps)
+            nc.vector.tensor_scalar(by_n5[:], window[b][:].indirect(l5[:]), -1.0, 0.0, ALU.mult, ALU.add)
+            by_n6 = ring.tile([P, S], F32, name="by_n6", bufs=last_steps)
+            nc.vector.tensor_tensor(by_n6[:], window[b][:].indirect(l6[:]), by_n5[:], ALU.add)
+            excess = ring.tile([P, S], F32, name="excess")
+            nc.scalar.activation(excess[:], by_n6[:], ACT.Relu, scale=-1.0)
+            total = bank("total", MIDDLE_BANK + b)
+            turn_sum(total, blocks_of(window[b], by_n5, excess))
+            total_turned = ring.tile([P, S], F32, name="total_turned")
+            nc.scalar.activation(total_turned[:], total[:], ACT.Copy)
+            total_upright = bank("total_upright", RETURN_BANK + b % 2)
+            turn_sum(total_upright, blocks_of(total_turned))
+            result = ring.tile([P, S], F32, name="result_of_scalar")
+            nc.scalar.activation(result[:], total_upright[:], ACT.Copy)
+            nc.scalar.dma_start(out_rows[b], result[:])
+
+        def finish_on_vector(b, c0, c1):
+            by_n5 = ring.tile([P, c1 - c0], F32, name="by_n5", bufs=last_steps)
+            by_n6 = ring.tile([P, c1 - c0], F32, name="by_n6", bufs=last_steps)
+            result = ring.tile([P, c1 - c0], F32, name="result_of_vector", bufs=last_steps)
+            nc.vector.tensor_tensor(by_n5[:], window[b][:].indirect(l5[:, c0 // 16:c1 // 16]), s_plain[b][:, c0:c1], ALU.add)
+            nc.vector.tensor_tensor(by_n6[:], window[b][:].indirect(l6[:, c0 // 16:c1 // 16]), s_plain[b][:, c0:c1], ALU.add)
+            nc.vector.tensor_tensor(result[:], by_n5[:], by_n6[:], ALU.max)
+            nc.sync.dma_start(out_rows[b][:, :, c0:c1], result[:])
 
         second_product(0)
-        for b in range(1, 4):
-            inverse(b)
+        for b in range(1, TILES):
+            invert(b)
             first_factor(b)
-            if b < 3:
-                products(b + 1)
+            if b + 1 < TILES:
+                weigh(b + 1)
             quantise_first(b)
             second_product(b)
-        for b in range(3):
-            finish(b, 1)
-        finish(3, 2)
+        for b in range(TURNED_BLOCKS):
+            finish_turned(b)
+        for b in range(TURNED_BLOCKS, TILES - 1):
+            finish_on_vector(b, 0, S)
+        finish_on_vector(TILES - 1, 0, HALF)
+        finish_on_vector(TILES - 1, HALF, S)

from contextlib import ExitStack

import concourse.mybir as mybir
from concourse.masks import make_identity

F32 = mybir.dt.float32
BF16 = mybir.dt.bfloat16
I32 = mybir.dt.int32
U32 = mybir.dt.uint32
U16 = mybir.dt.uint16
U8 = mybir.dt.uint8
FP8X4 = mybir.dt.float8_e4m3fn_x4
ALU = mybir.AluOpType
ACT = mybir.ActivationFunctionType

P = 128
T = 2048
S = 512
HALF = S // 2
TILES = 4
RUN = 8
WINDOW = 2 * S
FLOPS = 2 * 2 * 512 * 512 * 512

VECTOR_DIFFERENCE = (1, 1)
TURNED_BLOCKS = 2
VECTOR_CASTS = 2

PRODUCT_BANK, MIDDLE_BANK, RETURN_BANK = 0, 2, 6


def tile_picked_selfkernfracunder_none_p_kernel(
    tc, x_words, x_scales, w1, ga, gb, offs, n1, n2, n3, n4, n5, n6, out
):
    nc = tc.nc
    with ExitStack() as ctx:
        keep = ctx.enter_context(tc.tile_pool(name="keep", bufs=1))
        ring = ctx.enter_context(tc.tile_pool(name="ring", bufs=2))
        psum = ctx.enter_context(tc.psum_pool(name="psum", bufs=1))

        def bank(name, number):
            return psum.tile([P, S], F32, name=name, tag="bank%d" % number)

        def load_list(name, src):
            tile = keep.tile([P, S // 16], U16, name=name)
            nc.sync.dma_start(tile[:], src)
            return tile

        def load_gain(name, src):
            columns = []
            for t in range(TILES):
                column = keep.tile([P, 1], F32, name="%s%d" % (name, t))
                with nc.allow_non_contiguous_dma(reason="one value a partition"):
                    nc.sync.dma_start(column[:], src.rearrange("(g t a) o -> t g a o", t=TILES, a=RUN)[t])
                columns.append(column)
            return columns

        def turn_sum(dst, terms_of_block):
            for c, terms in enumerate(terms_of_block):
                for place, term in enumerate(terms):
                    nc.tensor.matmul(dst[:, c * P:(c + 1) * P], term, ident[:], is_transpose=True,
                                     start=(place == 0), stop=(place == len(terms) - 1))

        def blocks_of(*tiles):
            return [[tile[:, c * P:(c + 1) * P] for tile in tiles] for c in range(TILES)]

        def pairs_of(tiles):
            return [[tile[:, i, :] for i in range(2)] for tile in tiles]

        x_scale_rows = keep.tile([P, T], U8, name="x_scale_rows")
        nc.gpsimd.memset(x_scale_rows[:].bitcast(I32), 0)
        l_offs = load_list("l_offs", offs)
        for quad in range(4):
            nc.sync.dma_start(x_scale_rows[32 * quad:32 * quad + 4, :].bitcast(I32),
                              x_scales[0, 4 * quad:4 * quad + 4, :].bitcast(I32))
        w_raw = keep.tile([P, 4, S], F32, name="w_raw")
        nc.sync.dma_start(w_raw[:], w1.rearrange("(p j) c -> p j c", j=4))
        x_table = keep.tile([P, T], I32, name="x_table")
        nc.sync.dma_start(x_table[:], x_words[0].rearrange("p token j -> p (token j)").bitcast(I32))
        l1 = load_list("l1", n1)
        l2 = load_list("l2", n2)
        l4 = load_list("l4", n4)
        l3 = load_list("l3", n3)
        ga_t = load_gain("ga", ga)
        gb_t = load_gain("gb", gb)
        l5 = load_list("l5", n5)
        l6 = load_list("l6", n6)

        ident = keep.tile([P, P], F32, name="ident")
        make_identity(nc, ident[:])
        window = [keep.tile([P, WINDOW], F32, name="window%d" % t) for t in range(TILES)]
        for t in range(TILES):
            nc.vector.memset(window[t][:, S:], 0.0)

        x_s = keep.tile([P, S], U8, name="x_s", align_bytes=64)
        nc.vector.tensor_copy(x_s[:], x_scale_rows[:].indirect(l_offs[:]))
        w_c, w_s = [], []
        w_dealt = w_raw[:].rearrange("p j (g t a) -> p t g a j", t=TILES, a=RUN)
        for t in range(TILES):
            w_bf = keep.tile([P, S], BF16, name="w_bf%d" % t, align_bytes=64)
            w_bf_view = w_bf[:].rearrange("p (g a j) -> p g a j", a=RUN, j=4)
            if t < VECTOR_CASTS:
                nc.vector.tensor_copy(w_bf_view, w_dealt[:, t])
            else:
                nc.scalar.activation(w_bf_view, w_dealt[:, t], ACT.Copy)
            w_c.append(keep.tile([P, P], U32, name="w_c%d" % t, align_bytes=64))
            w_s.append(keep.tile([P, P], U8, name="w_s%d" % t, align_bytes=64))
            nc.vector.quantize_mx(out=w_c[t][:].bitcast(FP8X4), scales=w_s[t][:], in_=w_bf[:])
        x_c = keep.tile([P, S], U32, name="x_c", align_bytes=64)
        for h in range(2):
            nc.vector.tensor_copy(x_c[:, h * HALF:(h + 1) * HALF],
                                  x_table[:].bitcast(U32).indirect(l_offs[:, h * HALF // 16:(h + 1) * HALF // 16]))

        y_plain = [keep.tile([P, S], F32, name="y_plain%d" % t) for t in range(TILES)]
        passes = [(0, 0, HALF), (0, HALF, S)] + [(t, 0, S) for t in range(1, TILES)]
        for number, (t, c0, c1) in enumerate(passes):
            acc = bank("y_acc", PRODUCT_BANK + number % 2)
            nc.tensor.matmul_mx(out=acc[:, :c1 - c0], lhsT=w_c[t][:].bitcast(FP8X4), lhsT_scale=w_s[t][:],
                                rhs=x_c[:, c0:c1].bitcast(FP8X4), rhs_scale=x_s[:, c0:c1], start=True, stop=True)
            nc.scalar.activation(window[t][:, c0:c1], acc[:, :c1 - c0], ACT.Copy)
            if c1 == S:
                nc.sync.dma_start(y_plain[t][:], window[t][:, :S])

        neg = [keep.tile([P, 2, S], F32, name="neg%d" % t) for t in range(TILES)]
        kr = [keep.tile([P, TILES, 2, P], F32, name="kr%d" % t) for t in range(TILES)]
        turns = 0
        for t in range(TILES):
            for i, lst in enumerate((l1, l2)):
                nc.vector.tensor_scalar(neg[t][:, i, :], window[t][:].indirect(lst[:]), -1.0, 0.0, ALU.mult, ALU.add)
                square = keep.tile([P, S], F32, name="square%d_%d" % (t, i), tag="square%d" % i)
                if (t, i) == VECTOR_DIFFERENCE:
                    diff = keep.tile([P, S], F32, name="diff")
                    nc.vector.tensor_tensor(diff[:], neg[t][:, i, :], window[t][:, :S], ALU.add)
                    nc.scalar.activation(square[:], diff[:], ACT.Square)
                    upright = square
                else:
                    diff_turned = bank("diff_turned", MIDDLE_BANK + turns % 2)
                    turn_sum(diff_turned, blocks_of(neg[t][:, i, :], window[t]))
                    nc.scalar.activation(square[:], diff_turned[:], ACT.Square)
                    upright = bank("square_upright", MIDDLE_BANK + 2 + turns % 2)
                    turn_sum(upright, blocks_of(square))
                    turns = turns + 1
                nc.scalar.activation(kr[t][:, :, i, :].rearrange("p b (g a) -> p b g a", a=RUN),
                                     upright[:].rearrange("p (g b a) -> p b g a", b=TILES, a=RUN), ACT.Exp, scale=-0.5)

        d4 = [keep.tile([P, S], F32, name="d4_%d" % t) for t in range(TILES)]
        for t in range(TILES):
            nc.vector.tensor_tensor(d4[t][:], window[t][:].indirect(l4[:]), y_plain[t][:], ALU.subtract)
        d3 = [keep.tile([P, S], F32, name="d3_%d" % t) for t in range(TILES)]
        for t in range(TILES):
            nc.vector.tensor_tensor(d3[t][:], window[t][:].indirect(l3[:]), y_plain[t][:], ALU.subtract)

        weighted_tags = ("weighted0", "d3_%d" % (TILES - 1), "inverse0", "inverse1")
        weighted = [None] * TILES

        def weigh(b):
            weighted[b] = keep.tile([P, TILES, 2, P], F32, name="weighted%d" % b, tag=weighted_tags[b])
            for t in range(TILES):
                nc.vector.scalar_tensor_tensor(
                    weighted[b][:, t].rearrange("p i (g a) -> p (i g) a", a=RUN),
                    neg[t][:].rearrange("p i (g b a) -> p b (i g) a", b=TILES, a=RUN)[:, b],
                    ga_t[t][:],
                    kr[t][:, b].rearrange("p i (g a) -> p (i g) a", a=RUN),
                    ALU.mult, ALU.mult)

        gap = keep.tile([P, TILES, S], F32, name="gap", tag="square0")
        gap_root = keep.tile([P, TILES, S], F32, name="gap_root", tag="square1")
        z2_planes = keep.tile([P, TILES, S], BF16, name="z2_planes")

        def second_factor(t):
            nc.scalar.activation(gap[:, t, :], d4[t][:], ACT.Abs)
            nc.scalar.activation(gap_root[:, t, :], gap[:, t, :], ACT.Abs_reciprocal_sqrt, bias=0.5)
            gap_inverse = ring.tile([P, S], F32, name="gap_inverse", bufs=TILES)
            nc.scalar.activation(gap_inverse[:], gap_root[:, t, :], ACT.Square)
            nc.vector.scalar_tensor_tensor(z2_planes[:, t, :], d3[t][:], gb_t[t][:], gap_inverse[:], ALU.mult, ALU.mult)

        inverse = [None] * TILES

        def invert(b):
            den = bank("den", MIDDLE_BANK + b)
            turn_sum(den, pairs_of([kr[t][:, b] for t in range(TILES)]))
            den_root = ring.tile([P, S], F32, name="den_root")
            nc.scalar.activation(den_root[:].rearrange("q (u p e) -> q u p e", u=2, e=2),
                                 den[:].rearrange("q (u e p) -> q u p e", u=2, e=2), ACT.Abs_reciprocal_sqrt, bias=0.5)
            inverse[b] = keep.tile([P, S], F32, name="inverse%d" % b)
            nc.scalar.activation(inverse[b][:], den_root[:], ACT.Square)

        z_c = [keep.tile([P, P], U32, name="z_c%d" % b, align_bytes=64) for b in range(TILES)]
        z_s = [keep.tile([P, P], U8, name="z_s%d" % b, align_bytes=64) for b in range(TILES)]
        z_bf = [None] * TILES

        def first_factor(b):
            num = bank("num", MIDDLE_BANK + b)
            turn_sum(num, pairs_of([weighted[b][:, t] for t in range(TILES)]))
            z_turned = ring.tile([P, S], BF16, name="z_turned")
            nc.vector.tensor_tensor(z_turned[:].rearrange("q (u p e) -> q u p e", u=2, e=2),
                                    num[:].rearrange("q (u e p) -> q u p e", u=2, e=2),
                                    inverse[b][:].rearrange("q (u p e) -> q u p e", u=2, e=2), ALU.mult)
            z_words = bank("z_words", RETURN_BANK + b % 2)
            for u in range(2):
                nc.tensor.transpose(z_words[:, u * P:(u + 1) * P], z_turned[:].bitcast(F32)[:, u * P:(u + 1) * P], ident[:])
            z_bf[b] = ring.tile([P, S], BF16, name="z_bf", align_bytes=64)
            nc.scalar.copy(z_bf[b][:].bitcast(F32).rearrange("p (q u) -> p q u", u=2),
                           z_words[:, :2 * P].rearrange("p (u q) -> p q u", u=2))

        def quantise_first(b):
            nc.vector.quantize_mx(out=z_c[b][:].bitcast(FP8X4), scales=z_s[b][:], in_=z_bf[b][:])

        weigh(0)
        for t in range(TILES):
            second_factor(t)
        invert(0)
        z2_bf = keep.tile([P, S * TILES], BF16, name="z2_bf", align_bytes=64)
        z2_c = keep.tile([P, S], U32, name="z2_c", align_bytes=64)
        z2_s = keep.tile([P, S], U8, name="z2_s", align_bytes=64)
        first_factor(0)
        for h in range(2):
            nc.scalar.copy(
                z2_bf[:, h * HALF * TILES:(h + 1) * HALF * TILES].rearrange("p (c near t) -> p c t near", near=4, t=TILES),
                z2_planes[:, :, h * HALF:(h + 1) * HALF].rearrange("p t (c near) -> p c t near", near=4))
        weigh(1)
        quantise_first(0)
        for h in range(2):
            nc.vector.quantize_mx(out=z2_c[:, h * HALF:(h + 1) * HALF].bitcast(FP8X4), scales=z2_s[:, h * HALF:(h + 1) * HALF],
                                  in_=z2_bf[:, h * HALF * TILES:(h + 1) * HALF * TILES])

        s_plain = [None] * TILES
        out_rows = out.rearrange("(g b a) column -> b g a column", b=TILES, a=RUN)
        last_steps = TILES + 1

        def second_product(b):
            acc = bank("s_acc", PRODUCT_BANK + b % 2)
            nc.tensor.matmul_mx(out=acc[:], lhsT=z_c[b][:].bitcast(FP8X4), lhsT_scale=z_s[b][:],
                                rhs=z2_c[:].bitcast(FP8X4), rhs_scale=z2_s[:], start=True, stop=True)
            if b < TURNED_BLOCKS:
                nc.scalar.activation(window[b][:, :S], acc[:], ACT.Copy, scale=0.0625)
            else:
                nc.scalar.activation(window[b][:, :S], acc[:], ACT.Copy, scale=-0.0625)
                s_plain[b] = ring.tile([P, S], F32, name="s_plain", bufs=TILES)
                nc.scalar.activation(s_plain[b][:], acc[:], ACT.Copy, scale=0.0625)

        def finish_turned(b):
            by_n5 = ring.tile([P, S], F32, name="by_n5", bufs=last_steps)
            nc.vector.tensor_scalar(by_n5[:], window[b][:].indirect(l5[:]), -1.0, 0.0, ALU.mult, ALU.add)
            by_n6 = ring.tile([P, S], F32, name="by_n6", bufs=last_steps)
            nc.vector.tensor_tensor(by_n6[:], window[b][:].indirect(l6[:]), by_n5[:], ALU.add)
            excess = ring.tile([P, S], F32, name="excess")
            nc.scalar.activation(excess[:], by_n6[:], ACT.Relu, scale=-1.0)
            total = bank("total", MIDDLE_BANK + b)
            turn_sum(total, blocks_of(window[b], by_n5, excess))
            total_turned = ring.tile([P, S], F32, name="total_turned")
            nc.scalar.activation(total_turned[:], total[:], ACT.Copy)
            total_upright = bank("total_upright", RETURN_BANK + b % 2)
            turn_sum(total_upright, blocks_of(total_turned))
            result = ring.tile([P, S], F32, name="result_of_scalar")
            nc.scalar.activation(result[:], total_upright[:], ACT.Copy)
            nc.scalar.dma_start(out_rows[b], result[:])

        def finish_on_vector(b, c0, c1):
            by_n5 = ring.tile([P, c1 - c0], F32, name="by_n5", bufs=last_steps)
            by_n6 = ring.tile([P, c1 - c0], F32, name="by_n6", bufs=last_steps)
            result = ring.tile([P, c1 - c0], F32, name="result_of_vector", bufs=last_steps)
            nc.vector.tensor_tensor(by_n5[:], window[b][:].indirect(l5[:, c0 // 16:c1 // 16]), s_plain[b][:, c0:c1], ALU.add)
            nc.vector.tensor_tensor(by_n6[:], window[b][:].indirect(l6[:, c0 // 16:c1 // 16]), s_plain[b][:, c0:c1], ALU.add)
            nc.vector.tensor_tensor(result[:], by_n5[:], by_n6[:], ALU.max)
            nc.sync.dma_start(out_rows[b][:, :, c0:c1], result[:])

        second_product(0)
        for b in range(1, TILES):
            invert(b)
            first_factor(b)
            if b + 1 < TILES:
                weigh(b + 1)
            quantise_first(b)
            second_product(b)
        for b in range(TURNED_BLOCKS):
            finish_turned(b)
        for b in range(TURNED_BLOCKS, TILES - 1):
            finish_on_vector(b, 0, S)
        finish_on_vector(TILES - 1, 0, HALF)
        finish_on_vector(TILES - 1, HALF, S)
